import numpy as np
import ml_dtypes


def mxq(x, axis, fmt="e4m3"):
    dtype, down = {"e4m3": (ml_dtypes.float8_e4m3fn, 7), "e5m2": (ml_dtypes.float8_e5m2, 14)}[fmt]
    v = np.moveaxis(np.asarray(x, np.float32).astype(ml_dtypes.bfloat16).astype(np.float64), axis, -1)
    blocks = v.reshape(v.shape[:-1] + (-1, 32))
    amax = np.abs(blocks).max(-1, keepdims=True)
    byte = np.maximum(np.where(amax > 0, np.frexp(amax)[1] - 1 + 127, 0) - down, 1)
    scale = np.exp2(byte - 127.0)
    codes = (blocks / scale).astype(np.float32).astype(dtype).astype(np.float64)
    return np.moveaxis((codes * scale).reshape(v.shape), -1, axis)


WIDE = False


def mx_kscale(k):
    if not WIDE:
        return np.ones(k)
    levels = np.array([10, -10, 5, -5, 0])
    if k % 512:
        return np.exp2(np.random.permutation(np.resize(levels, k // 32))).repeat(32)
    a = np.empty((k // 512, 16))
    for p in range(k // 512):
        a[p, :8] = np.random.permutation(np.resize(levels, 8))
        for g in range(8):
            far = levels[np.abs(levels - a[p, g]) >= 10]
            a[p, g + 8] = far[np.random.randint(len(far))]
    return np.exp2(a.ravel()).repeat(32)


def f64(x):
    return np.asarray(x).astype(np.float64)


def striped(idx):
    return np.tile(np.asarray(idx).reshape(-1, 16).T, (8, 1)).astype(np.uint16)


def unstriped(offs):
    return offs[:16].T.reshape(-1).astype(np.int64)


B, N, T, D, DV, NQ = 1, 2048, 4096, 512, 512, 128
PAGE = 128


def setup_inputs():
    n = np.random.standard_normal
    pages = np.random.permutation(T // PAGE)[:B * N // PAGE]
    idx = (pages[:, None] * PAGE + np.arange(PAGE)[None, :]).reshape(-1)
    s = mx_kscale(D)[:, None]
    u = np.ones(T)
    u[idx] = mx_kscale(B * N)
    r = np.random.uniform(0.5, 2.0, T)
    raw = n((D, T)) / s / (u * r)
    return {
        "qT": (n((B, D, NQ)) * s * (0.90 / np.sqrt(D))).astype(np.float32),
        "cT": raw.astype(np.float32),
        "ts": np.tile(u * r, (128, 1)).astype(np.float32),
        "ch": np.tile(s[:, 0] * np.random.uniform(0.5, 2.0, D), (128, 1)).astype(np.float32),
        "offs": striped(idx),
    }


def reference(qT, cT, ts, ch, offs):
    idx = unstriped(offs)
    c = f64(cT)
    pick = lambda x: x[:, idx].reshape(x.shape[0], B, N).transpose(1, 0, 2)
    q = f64(qT)
    score = mxq(q, 1, "e4m3").transpose(0, 2, 1) @ mxq(pick(c), 1, "e4m3")
    score = score * pick(f64(ts))[:, :1, :]
    m = score.max(-1, keepdims=True)
    p = np.exp(score - m)
    total = p.sum(-1, keepdims=True)
    w = p * pick(f64(ts))[:, :1, :]
    y = mxq(w, 2, "e4m3") @ mxq(pick(c).transpose(0, 2, 1), 1, "e4m3")
    y = y / total
    y = y * f64(ch)[:1]
    return y

@@ -1,0 +1,233 @@
+from contextlib import ExitStack
+
+import concourse.mybir as mybir
+from concourse.masks import make_identity
+
+F32 = mybir.dt.float32
+BF16 = mybir.dt.bfloat16
+U32 = mybir.dt.uint32
+U16 = mybir.dt.uint16
+U8 = mybir.dt.uint8
+FP8X4 = mybir.dt.float8_e4m3fn_x4
+ALU = mybir.AluOpType
+ACT = mybir.ActivationFunctionType
+AX = mybir.AxisListType
+
+P = 128
+T = 4096
+N = 2048
+D = 512
+NQ = 128
+PASS = 512
+PASSES = N // PASS
+FLOPS = 2 * 2 * NQ * N * D
+
+LOAD_WIDTHS = ((2048, 2048), (2048, 1024, 512, 256, 256))
+VECTOR_EIGHTHS = 5
+
+
+def tile_attend_mla_long_kernel(tc, qT, cT, ts, ch, offs, out):
+    nc = tc.nc
+    with ExitStack() as ctx:
+        lists = ctx.enter_context(tc.tile_pool(name="lists", bufs=1))
+        keep = ctx.enter_context(tc.tile_pool(name="keep", bufs=1))
+        ring = ctx.enter_context(tc.tile_pool(name="ring", bufs=3))
+        rows = ctx.enter_context(tc.tile_pool(name="rows", bufs=2))
+        turn = ctx.enter_context(tc.psum_pool(name="turn", bufs=4))
+        score = ctx.enter_context(tc.psum_pool(name="score", bufs=3))
+        acc = ctx.enter_context(tc.psum_pool(name="acc", bufs=1))
+
+        offsets = lists.tile([P, N // 16], U16, name="offsets")
+        nc.sync.dma_start(offsets[:], offs)
+
+        ts_window = keep.tile([P, T], F32, name="ts_window")
+        nc.vector.memset(ts_window[:], 0.0)
+
+        pool_rows = cT.rearrange("(p u h) t -> u p h t", u=2, h=2)
+        raws = []
+        for u in range(2):
+            c0 = 0
+            for k, w in enumerate(LOAD_WIDTHS[u]):
+                raw = keep.tile([P, 2, w], F32, name="raw%d_%d" % (u, k))
+                nc.sync.dma_start(raw[:], pool_rows[u][:, :, c0:c0 + w])
+                raws.append((u, c0, w, raw))
+                c0 += w
+                if (u, k) == (0, 0):
+                    nc.sync.dma_start(ts_window[0:1, :], ts[0:1, :])
+        q_raw = keep.tile([P, 4, NQ], F32, name="q_raw")
+        nc.sync.dma_start(q_raw[:], qT[0].rearrange("(p t) n -> p t n", t=4))
+        ch_sb = keep.tile([P, D], F32, name="ch_sb")
+        nc.sync.dma_start(ch_sb[:], ch)
+
+        ident = keep.tile([P, P], F32, name="ident")
+        make_identity(nc, ident[:])
+        warm = keep.tile([P, 8], F32, name="warm")
+        nc.vector.memset(warm[:], 0.0)
+        warm_out = keep.tile([P, 8], F32, name="warm_out")
+        nc.scalar.activation(warm_out[:], warm[:], ACT.Exp)
+
+        ts_listed = rows.tile([P, N], F32, name="ts_listed", tag="row")
+        nc.vector.tensor_copy(ts_listed[:], ts_window[:].indirect(offsets[:]))
+        ts_placed = rows.tile([P, N], F32, name="ts_placed", tag="row")
+        for g in range(PASSES):
+            cols = slice(g * PASS, (g + 1) * PASS)
+            nc.vector.tensor_copy(
+                ts_placed[:, cols].rearrange("p (j b r) -> p j b r", j=4, r=8),
+                ts_listed[:, cols].rearrange("p (b j r) -> p j b r", j=4, r=8),
+            )
+        ts_part = keep.tile([P, PASSES, 4], F32, name="ts_part")
+        ts_free = keep.tile([P, N], F32, name="ts_free")
+        for g in range(PASSES):
+            bank = turn.tile([P, 4, P], F32, name="bank", tag="turn")
+            for j in range(4):
+                c = g * PASS + j * P
+                nc.tensor.transpose(bank[:, j, :], ts_placed[:, c:c + P], ident[:])
+            nc.scalar.copy(ts_part[:, g, :], bank[:, :, 0])
+        for g in range(PASSES):
+            bank = turn.tile([P, 4, P], F32, name="bank", tag="turn")
+            for j in range(4):
+                nc.tensor.transpose(bank[:, j, :], ts_part[:, g, j:j + 1].to_broadcast([P, P]), ident[:])
+            nc.scalar.copy(ts_free[:, g * PASS:(g + 1) * PASS], bank[:].rearrange("p j s -> p (j s)"))
+
+        windows = [keep.tile([P, 2 * T], BF16, name="window%d" % u) for u in range(2)]
+        listed = keep.tile([P, 2, N], U32, name="listed")
+        v_codes = keep.tile([P, PASSES, D], U32, name="v_codes", align_bytes=64)
+        v_scales = keep.tile([P, PASSES, D], U8, name="v_scales", align_bytes=64)
+
+        def cast(u):
+            pairs = windows[u][:].rearrange("p (t h) -> p t h", h=2)
+            for ru, c0, w, raw in raws:
+                if ru == u:
+                    cut = w * VECTOR_EIGHTHS // 8
+                    src = raw[:].rearrange("p h t -> p t h")
+                    nc.vector.tensor_copy(pairs[:, c0:c0 + cut, :], src[:, 0:cut, :])
+                    nc.scalar.copy(pairs[:, c0 + cut:c0 + w, :], src[:, cut:w, :])
+
+        def gather(u, g):
+            nc.vector.tensor_copy(
+                listed[:, u, g * PASS:(g + 1) * PASS].rearrange("p (j b r) -> p b j r", j=4, r=8),
+                windows[u][:].bitcast(U32).indirect(offsets[:, g * 32:(g + 1) * 32]),
+            )
+
+        def turn_values(u, g):
+            bank = turn.tile([P, 4, P], F32, name="bank", tag="turn")
+            words = listed[:, u, :].bitcast(F32)
+            for j in range(4):
+                c = g * PASS + j * P
+                nc.tensor.transpose(bank[:, j, :], words[:, c:c + P], ident[:])
+            v_bf = ring.tile([P, 2 * P, 4], BF16, name="v_bf", align_bytes=64)
+            nc.scalar.copy(v_bf[:], bank[:].bitcast(BF16).rearrange("s j e -> s e j"))
+            return v_bf
+
+        def quantise_values(u, g, v_bf):
+            cols = slice(u * 2 * P, (u + 1) * 2 * P)
+            nc.vector.quantize_mx(
+                out=v_codes[:, g, cols].bitcast(FP8X4),
+                scales=v_scales[:, g, cols],
+                in_=v_bf[:].rearrange("s e j -> s (e j)"),
+            )
+
+        cast(0)
+        for g in range(PASSES):
+            gather(0, g)
+        for g in range(PASSES):
+            quantise_values(0, g, turn_values(0, g))
+        cast(1)
+        for g in range(PASSES):
+            gather(1, g)
+
+        q_bf = keep.tile([P, NQ, 4], BF16, name="q_bf", align_bytes=64)
+        nc.scalar.copy(q_bf[:], q_raw[:].rearrange("p t n -> p n t"))
+        q_codes = keep.tile([P, NQ], U32, name="q_codes", align_bytes=64)
+        q_scales = keep.tile([P, NQ], U8, name="q_scales", align_bytes=64)
+        nc.vector.quantize_mx(
+            out=q_codes[:].bitcast(FP8X4), scales=q_scales[:], in_=q_bf[:].rearrange("p n t -> p (n t)")
+        )
+
+        k_codes = keep.tile([P, N], U32, name="k_codes", align_bytes=64)
+        k_scales = keep.tile([P, N], U8, name="k_scales", align_bytes=64)
+        a = rows.tile([P, N], F32, name="a", tag="row")
+        p = rows.tile([P, N], F32, name="p", tag="row")
+        neg_max = keep.tile([P, PASSES], F32, name="neg_max")
+        for g in range(PASSES):
+            cols = slice(g * PASS, (g + 1) * PASS)
+            k_words = ring.tile([P, PASS, 2], U32, name="k_words", align_bytes=64)
+            nc.scalar.copy(k_words[:], listed[:, :, cols].rearrange("p u s -> p s u"))
+            nc.vector.quantize_mx(
+                out=k_codes[:, cols].bitcast(FP8X4),
+                scales=k_scales[:, cols],
+                in_=k_words[:].rearrange("p s u -> p (s u)").bitcast(BF16),
+            )
+            s_bank = score.tile([P, PASS], F32, name="s_bank")
+            nc.tensor.matmul_mx(
+                out=s_bank[:],
+                lhsT=q_codes[:].bitcast(FP8X4),
+                lhsT_scale=q_scales[:],
+                rhs=k_codes[:, cols].bitcast(FP8X4),
+                rhs_scale=k_scales[:, cols],
+                start=True,
+                stop=True,
+            )
+            nc.vector.tensor_tensor(a[:, cols], s_bank[:], ts_free[:, cols], ALU.mult)
+            nc.vector.tensor_scalar(
+                out=p[:, cols],
+                in0=a[:, cols],
+                scalar1=-1.0,
+                scalar2=neg_max[:, g - 1:g] if g else None,
+                op0=ALU.mult,
+                op1=ALU.min,
+                accum_out=neg_max[:, g:g + 1],
+            )
+
+        for g in range(PASSES):
+            quantise_values(1, g, turn_values(1, g))
+
+        sums = keep.tile([P, PASSES], F32, name="sums")
+        w_codes = keep.tile([P, PASSES, NQ], U32, name="w_codes", align_bytes=64)
+        w_scales = keep.tile([P, PASSES, NQ], U8, name="w_scales", align_bytes=64)
+        y = acc.tile([P, D], F32, name="y")
+        for g in range(PASSES):
+            cols = slice(g * PASS, (g + 1) * PASS)
+            nc.scalar.activation(
+                p[:, cols], a[:, cols], ACT.Exp, bias=neg_max[:, PASSES - 1:PASSES], accum_out=sums[:, g:g + 1]
+            )
+            bank = turn.tile([P, 4, P], F32, name="bank", tag="turn")
+            for j in range(4):
+                c = g * PASS + j * P
+                nc.tensor.transpose(bank[:, j, :], p[:, c:c + P], ident[:])
+            w_bf = ring.tile([P, NQ, 4], BF16, name="w_bf", align_bytes=64)
+            nc.vector.tensor_tensor(
+                w_bf[:],
+                bank[:].rearrange("s j q -> s q j"),
+                ts_part[:, g:g + 1, :].to_broadcast([P, NQ, 4]),
+                ALU.mult,
+            )
+            nc.vector.quantize_mx(
+                out=w_codes[:, g, :].bitcast(FP8X4),
+                scales=w_scales[:, g, :],
+                in_=w_bf[:].rearrange("s q j -> s (q j)"),
+            )
+            nc.tensor.matmul_mx(
+                out=y[:],
+                lhsT=w_codes[:, g, :].bitcast(FP8X4),
+                lhsT_scale=w_scales[:, g, :],
+                rhs=v_codes[:, g, :].bitcast(FP8X4),
+                rhs_scale=v_scales[:, g, :],
+                start=(g == 0),
+                stop=(g == PASSES - 1),
+            )
+
+        total = keep.tile([P, 1], F32, name="total")
+        nc.vector.tensor_reduce(total[:], sums[:], AX.X, ALU.add)
+        inverse = keep.tile([P, 1], F32, name="inverse")
+        nc.vector.reciprocal(inverse[:], total[:])
+        factor = keep.tile([P, D], F32, name="factor")
+        nc.scalar.activation(factor[:], ch_sb[:], ACT.Copy, scale=inverse[:])
+        result = keep.tile([P, D], F32, name="result")
+        nc.vector.tensor_tensor(
+            result[:].rearrange("q (c u h) -> q c u h", u=2, h=2),
+            y[:].rearrange("q (u c h) -> q c u h", u=2, h=2),
+            factor[:].rearrange("q (c u h) -> q c u h", u=2, h=2),
+            ALU.mult,
+        )
+        nc.sync.dma_start(out[0], result[:])

@@ -22,8 +22,9 @@ PASS = 512
 PASSES = N // PASS
 FLOPS = 2 * 2 * NQ * N * D
 
-LOAD_WIDTHS = ((2048, 2048), (2048, 1024, 512, 256, 256))
-VECTOR_EIGHTHS = 5
+LOAD_WIDTHS = ((1024, 1024, 1024, 512, 512), (1024, 1024, 1024, 512, 256, 256))
+VALUES_BEFORE = (2, 3, 4, 6)
+VECTOR_SHARE = ((2, 2, 12, 11, 14), (6, 16, 16, 14, 16, 0))
 
 
 def tile_attend_mla_long_kernel(tc, qT, cT, ts, ch, offs, out):
@@ -32,6 +33,7 @@ def tile_attend_mla_long_kernel(tc, qT, cT, ts, ch, offs, out):
         lists = ctx.enter_context(tc.tile_pool(name="lists", bufs=1))
         keep = ctx.enter_context(tc.tile_pool(name="keep", bufs=1))
         ring = ctx.enter_context(tc.tile_pool(name="ring", bufs=3))
+        stage = ctx.enter_context(tc.tile_pool(name="stage", bufs=4))
         rows = ctx.enter_context(tc.tile_pool(name="rows", bufs=2))
         turn = ctx.enter_context(tc.psum_pool(name="turn", bufs=4))
         score = ctx.enter_context(tc.psum_pool(name="score", bufs=3))
@@ -50,7 +52,7 @@ def tile_attend_mla_long_kernel(tc, qT, cT, ts, ch, offs, out):
             for k, w in enumerate(LOAD_WIDTHS[u]):
                 raw = keep.tile([P, 2, w], F32, name="raw%d_%d" % (u, k))
                 nc.sync.dma_start(raw[:], pool_rows[u][:, :, c0:c0 + w])
-                raws.append((u, c0, w, raw))
+                raws.append((u, k, c0, w, raw))
                 c0 += w
                 if (u, k) == (0, 0):
                     nc.sync.dma_start(ts_window[0:1, :], ts[0:1, :])
@@ -66,42 +68,52 @@ def tile_attend_mla_long_kernel(tc, qT, cT, ts, ch, offs, out):
         warm_out = keep.tile([P, 8], F32, name="warm_out")
         nc.scalar.activation(warm_out[:], warm[:], ACT.Exp)
 
-        ts_listed = rows.tile([P, N], F32, name="ts_listed", tag="row")
-        nc.vector.tensor_copy(ts_listed[:], ts_window[:].indirect(offsets[:]))
-        ts_placed = rows.tile([P, N], F32, name="ts_placed", tag="row")
-        for g in range(PASSES):
-            cols = slice(g * PASS, (g + 1) * PASS)
-            nc.vector.tensor_copy(
-                ts_placed[:, cols].rearrange("p (j b r) -> p j b r", j=4, r=8),
-                ts_listed[:, cols].rearrange("p (b j r) -> p j b r", j=4, r=8),
-            )
         ts_part = keep.tile([P, PASSES, 4], F32, name="ts_part")
         ts_free = keep.tile([P, N], F32, name="ts_free")
-        for g in range(PASSES):
-            bank = turn.tile([P, 4, P], F32, name="bank", tag="turn")
-            for j in range(4):
-                c = g * PASS + j * P
-                nc.tensor.transpose(bank[:, j, :], ts_placed[:, c:c + P], ident[:])
-            nc.scalar.copy(ts_part[:, g, :], bank[:, :, 0])
-        for g in range(PASSES):
-            bank = turn.tile([P, 4, P], F32, name="bank", tag="turn")
-            for j in range(4):
-                nc.tensor.transpose(bank[:, j, :], ts_part[:, g, j:j + 1].to_broadcast([P, P]), ident[:])
-            nc.scalar.copy(ts_free[:, g * PASS:(g + 1) * PASS], bank[:].rearrange("p j s -> p (j s)"))
 
-        windows = [keep.tile([P, 2 * T], BF16, name="window%d" % u) for u in range(2)]
+        def token_scales():
+            ts_listed = rows.tile([P, N], F32, name="ts_listed", tag="row")
+            ts_down = keep.tile([P, PASSES, 4], F32, name="ts_down")
+            for g in range(PASSES):
+                nc.vector.tensor_copy(
+                    ts_listed[:, g * PASS:(g + 1) * PASS], ts_window[:].indirect(offsets[:, g * 32:(g + 1) * 32])
+                )
+            for g in range(PASSES):
+                bank = turn.tile([P, 4, P], F32, name="bank", tag="turn")
+                for c in range(4):
+                    c0 = g * PASS + c * P
+                    nc.tensor.transpose(bank[:, c, :], ts_listed[:, c0:c0 + P], ident[:])
+                nc.scalar.copy(ts_down[:, g, :], bank[:, :, 0])
+            for g in range(PASSES):
+                bank = turn.tile([P, 4, P], F32, name="bank", tag="turn")
+                for c in range(4):
+                    nc.tensor.transpose(bank[:, c, :], ts_down[:, g, c:c + 1].to_broadcast([P, P]), ident[:])
+                nc.scalar.copy(
+                    ts_free[:, g * PASS:(g + 1) * PASS].rearrange("p (j b r) -> p j b r", j=4, r=8),
+                    bank[:].rearrange("p c (x j r) -> p j (c x) r", j=4, r=8),
+                )
+            for g in range(PASSES):
+                bank = turn.tile([P, 4, P], F32, name="bank", tag="turn")
+                for j in range(4):
+                    c0 = g * PASS + j * P
+                    nc.tensor.transpose(bank[:, j, :], ts_free[:, c0:c0 + P], ident[:])
+                nc.scalar.copy(ts_part[:, g, :], bank[:, :, 0])
+
+        windows = [keep.tile([P, 2 * T], BF16, name="window%d" % u, align_bytes=64) for u in range(2)]
         listed = keep.tile([P, 2, N], U32, name="listed")
         v_codes = keep.tile([P, PASSES, D], U32, name="v_codes", align_bytes=64)
         v_scales = keep.tile([P, PASSES, D], U8, name="v_scales", align_bytes=64)
 
-        def cast(u):
+        def cast(u, first, last):
             pairs = windows[u][:].rearrange("p (t h) -> p t h", h=2)
-            for ru, c0, w, raw in raws:
-                if ru == u:
-                    cut = w * VECTOR_EIGHTHS // 8
+            for ru, k, c0, w, raw in raws:
+                if ru == u and first <= k < last:
+                    cut = w * VECTOR_SHARE[u][k] // 16
                     src = raw[:].rearrange("p h t -> p t h")
-                    nc.vector.tensor_copy(pairs[:, c0:c0 + cut, :], src[:, 0:cut, :])
-                    nc.scalar.copy(pairs[:, c0 + cut:c0 + w, :], src[:, cut:w, :])
+                    if cut > 0:
+                        nc.vector.tensor_copy(pairs[:, c0:c0 + cut, :], src[:, 0:cut, :])
+                    if cut < w:
+                        nc.scalar.copy(pairs[:, c0 + cut:c0 + w, :], src[:, cut:w, :])
 
         def gather(u, g):
             nc.vector.tensor_copy(
@@ -115,7 +127,7 @@ def tile_attend_mla_long_kernel(tc, qT, cT, ts, ch, offs, out):
             for j in range(4):
                 c = g * PASS + j * P
                 nc.tensor.transpose(bank[:, j, :], words[:, c:c + P], ident[:])
-            v_bf = ring.tile([P, 2 * P, 4], BF16, name="v_bf", align_bytes=64)
+            v_bf = stage.tile([P, 2 * P, 4], BF16, name="v_bf", tag="stage", align_bytes=64)
             nc.scalar.copy(v_bf[:], bank[:].bitcast(BF16).rearrange("s j e -> s e j"))
             return v_bf
 
@@ -127,18 +139,21 @@ def tile_attend_mla_long_kernel(tc, qT, cT, ts, ch, offs, out):
                 in_=v_bf[:].rearrange("s e j -> s (e j)"),
             )
 
-        cast(0)
+        token_scales()
+        cast(0, 0, 9)
         for g in range(PASSES):
             gather(0, g)
-        for g in range(PASSES):
-            quantise_values(0, g, turn_values(0, g))
-        cast(1)
+        for k in range(len(LOAD_WIDTHS[1]) + 1):
+            for g in range(PASSES):
+                if VALUES_BEFORE[g] == k:
+                    quantise_values(0, g, turn_values(0, g))
+            cast(1, k, k + 1)
         for g in range(PASSES):
             gather(1, g)
 
         q_bf = keep.tile([P, NQ, 4], BF16, name="q_bf", align_bytes=64)
         nc.scalar.copy(q_bf[:], q_raw[:].rearrange("p t n -> p n t"))
-        q_codes = keep.tile([P, NQ], U32, name="q_codes", align_bytes=64)
+        q_codes = keep.tile([P, NQ], U32, name="q_codes", tag="window1", align_bytes=64)
         q_scales = keep.tile([P, NQ], U8, name="q_scales", align_bytes=64)
         nc.vector.quantize_mx(
             out=q_codes[:].bitcast(FP8X4), scales=q_scales[:], in_=q_bf[:].rearrange("p n t -> p (n t)")
@@ -149,9 +164,11 @@ def tile_attend_mla_long_kernel(tc, qT, cT, ts, ch, offs, out):
         a = rows.tile([P, N], F32, name="a", tag="row")
         p = rows.tile([P, N], F32, name="p", tag="row")
         neg_max = keep.tile([P, PASSES], F32, name="neg_max")
-        for g in range(PASSES):
+        s_banks = []
+
+        def scores(g):
             cols = slice(g * PASS, (g + 1) * PASS)
-            k_words = ring.tile([P, PASS, 2], U32, name="k_words", align_bytes=64)
+            k_words = stage.tile([P, PASS, 2], U32, name="k_words", tag="stage", align_bytes=64)
             nc.scalar.copy(k_words[:], listed[:, :, cols].rearrange("p u s -> p s u"))
             nc.vector.quantize_mx(
                 out=k_codes[:, cols].bitcast(FP8X4),
@@ -168,7 +185,14 @@ def tile_attend_mla_long_kernel(tc, qT, cT, ts, ch, offs, out):
                 start=True,
                 stop=True,
             )
-            nc.vector.tensor_tensor(a[:, cols], s_bank[:], ts_free[:, cols], ALU.mult)
+            s_banks.append(s_bank)
+
+        def scale_scores(g):
+            cols = slice(g * PASS, (g + 1) * PASS)
+            nc.vector.tensor_tensor(a[:, cols], s_banks[g][:], ts_free[:, cols], ALU.mult)
+
+        def row_max(g):
+            cols = slice(g * PASS, (g + 1) * PASS)
             nc.vector.tensor_scalar(
                 out=p[:, cols],
                 in0=a[:, cols],
@@ -179,18 +203,38 @@ def tile_attend_mla_long_kernel(tc, qT, cT, ts, ch, offs, out):
                 accum_out=neg_max[:, g:g + 1],
             )
 
-        for g in range(PASSES):
-            quantise_values(1, g, turn_values(1, g))
+        scores(0)
+        scores(1)
+        scores(2)
+        scale_scores(0)
+        scores(3)
+        for g in range(1, PASSES):
+            scale_scores(g)
+            row_max(g - 1)
+        row_max(PASSES - 1)
 
         sums = keep.tile([P, PASSES], F32, name="sums")
-        w_codes = keep.tile([P, PASSES, NQ], U32, name="w_codes", align_bytes=64)
-        w_scales = keep.tile([P, PASSES, NQ], U8, name="w_scales", align_bytes=64)
-        y = acc.tile([P, D], F32, name="y")
         for g in range(PASSES):
             cols = slice(g * PASS, (g + 1) * PASS)
             nc.scalar.activation(
                 p[:, cols], a[:, cols], ACT.Exp, bias=neg_max[:, PASSES - 1:PASSES], accum_out=sums[:, g:g + 1]
             )
+        for g in range(PASSES):
+            quantise_values(1, g, turn_values(1, g))
+
+        total = keep.tile([P, 1], F32, name="total")
+        nc.vector.tensor_reduce(total[:], sums[:], AX.X, ALU.add)
+        inverse = keep.tile([P, 1], F32, name="inverse")
+        nc.vector.reciprocal(inverse[:], total[:])
+        factor = keep.tile([P, D], F32, name="factor")
+        nc.scalar.activation(factor[:], ch_sb[:], ACT.Copy, scale=inverse[:])
+
+        w_codes = keep.tile([P, PASSES, NQ], U32, name="w_codes", align_bytes=64)
+        w_scales = keep.tile([P, PASSES, NQ], U8, name="w_scales", align_bytes=64)
+        y = acc.tile([P, D], F32, name="y")
+        w_tiles = []
+
+        def weights(g):
             bank = turn.tile([P, 4, P], F32, name="bank", tag="turn")
             for j in range(4):
                 c = g * PASS + j * P
@@ -202,10 +246,13 @@ def tile_attend_mla_long_kernel(tc, qT, cT, ts, ch, offs, out):
                 ts_part[:, g:g + 1, :].to_broadcast([P, NQ, 4]),
                 ALU.mult,
             )
+            w_tiles.append(w_bf)
+
+        def weighted_sum(g):
             nc.vector.quantize_mx(
                 out=w_codes[:, g, :].bitcast(FP8X4),
                 scales=w_scales[:, g, :],
-                in_=w_bf[:].rearrange("s q j -> s (q j)"),
+                in_=w_tiles[g][:].rearrange("s q j -> s (q j)"),
             )
             nc.tensor.matmul_mx(
                 out=y[:],
@@ -217,12 +264,12 @@ def tile_attend_mla_long_kernel(tc, qT, cT, ts, ch, offs, out):
                 stop=(g == PASSES - 1),
             )
 
-        total = keep.tile([P, 1], F32, name="total")
-        nc.vector.tensor_reduce(total[:], sums[:], AX.X, ALU.add)
-        inverse = keep.tile([P, 1], F32, name="inverse")
-        nc.vector.reciprocal(inverse[:], total[:])
-        factor = keep.tile([P, D], F32, name="factor")
-        nc.scalar.activation(factor[:], ch_sb[:], ACT.Copy, scale=inverse[:])
+        weights(0)
+        for g in range(1, PASSES):
+            weights(g)
+            weighted_sum(g - 1)
+        weighted_sum(PASSES - 1)
+
         result = keep.tile([P, D], F32, name="result")
         nc.vector.tensor_tensor(
             result[:].rearrange("q (c u h) -> q c u h", u=2, h=2),

@@ -105,15 +105,16 @@ def tile_attend_mla_long_kernel(tc, qT, cT, ts, ch, offs, out):
         v_scales = keep.tile([P, PASSES, D], U8, name="v_scales", align_bytes=64)
 
         def cast(u, first, last):
-            pairs = windows[u][:].rearrange("p (t h) -> p t h", h=2)
+            pairs = windows[u][:].rearrange("p (c i h) -> p c h i", i=2, h=2)
             for ru, k, c0, w, raw in raws:
                 if ru == u and first <= k < last:
-                    cut = w * VECTOR_SHARE[u][k] // 16
-                    src = raw[:].rearrange("p h t -> p t h")
+                    cut = w // 2 * VECTOR_SHARE[u][k] // 16
+                    src = raw[:].rearrange("p h (c i) -> p c h i", i=2)
+                    dst = pairs[:, c0 // 2:(c0 + w) // 2]
                     if cut > 0:
-                        nc.vector.tensor_copy(pairs[:, c0:c0 + cut, :], src[:, 0:cut, :])
-                    if cut < w:
-                        nc.scalar.copy(pairs[:, c0 + cut:c0 + w, :], src[:, cut:w, :])
+                        nc.vector.tensor_copy(dst[:, 0:cut], src[:, 0:cut])
+                    if cut < w // 2:
+                        nc.scalar.copy(dst[:, cut:], src[:, cut:])
 
         def gather(u, g):
             nc.vector.tensor_copy(
@@ -152,7 +153,9 @@ def tile_attend_mla_long_kernel(tc, qT, cT, ts, ch, offs, out):
             gather(1, g)
 
         q_bf = keep.tile([P, NQ, 4], BF16, name="q_bf", align_bytes=64)
-        nc.scalar.copy(q_bf[:], q_raw[:].rearrange("p t n -> p n t"))
+        nc.scalar.copy(
+            q_bf[:].rearrange("p (c i) t -> p c t i", i=2), q_raw[:].rearrange("p t (c i) -> p c t i", i=2)
+        )
         q_codes = keep.tile([P, NQ], U32, name="q_codes", tag="window1", align_bytes=64)
         q_scales = keep.tile([P, NQ], U8, name="q_scales", align_bytes=64)
         nc.vector.quantize_mx(
@@ -169,7 +172,10 @@ def tile_attend_mla_long_kernel(tc, qT, cT, ts, ch, offs, out):
         def scores(g):
             cols = slice(g * PASS, (g + 1) * PASS)
             k_words = stage.tile([P, PASS, 2], U32, name="k_words", tag="stage", align_bytes=64)
-            nc.scalar.copy(k_words[:], listed[:, :, cols].rearrange("p u s -> p s u"))
+            nc.scalar.copy(
+                k_words[:].rearrange("p (c i) u -> p c u i", i=2),
+                listed[:, :, cols].rearrange("p u (c i) -> p c u i", i=2),
+            )
             nc.vector.quantize_mx(
                 out=k_codes[:, cols].bitcast(FP8X4),
                 scales=k_scales[:, cols],

from contextlib import ExitStack

import concourse.mybir as mybir
from concourse.masks import make_identity

F32 = mybir.dt.float32
BF16 = mybir.dt.bfloat16
U32 = mybir.dt.uint32
U16 = mybir.dt.uint16
U8 = mybir.dt.uint8
FP8X4 = mybir.dt.float8_e4m3fn_x4
ALU = mybir.AluOpType
ACT = mybir.ActivationFunctionType
AX = mybir.AxisListType

P = 128
T = 4096
N = 2048
D = 512
NQ = 128
PASS = 512
PASSES = N // PASS
FLOPS = 2 * 2 * NQ * N * D

LOAD_WIDTHS = ((1024, 1024, 1024, 512, 512), (1024, 1024, 1024, 512, 256, 256))
VALUES_BEFORE = (2, 3, 4, 6)
VECTOR_SHARE = ((2, 2, 12, 11, 14), (6, 16, 16, 14, 16, 0))


def tile_attend_mla_long_kernel(tc, qT, cT, ts, ch, offs, out):
    nc = tc.nc
    with ExitStack() as ctx:
        lists = ctx.enter_context(tc.tile_pool(name="lists", bufs=1))
        keep = ctx.enter_context(tc.tile_pool(name="keep", bufs=1))
        ring = ctx.enter_context(tc.tile_pool(name="ring", bufs=3))
        stage = ctx.enter_context(tc.tile_pool(name="stage", bufs=4))
        rows = ctx.enter_context(tc.tile_pool(name="rows", bufs=2))
        turn = ctx.enter_context(tc.psum_pool(name="turn", bufs=4))
        score = ctx.enter_context(tc.psum_pool(name="score", bufs=3))
        acc = ctx.enter_context(tc.psum_pool(name="acc", bufs=1))

        offsets = lists.tile([P, N // 16], U16, name="offsets")
        nc.sync.dma_start(offsets[:], offs)

        ts_window = keep.tile([P, T], F32, name="ts_window")
        nc.vector.memset(ts_window[:], 0.0)

        pool_rows = cT.rearrange("(p u h) t -> u p h t", u=2, h=2)
        raws = []
        for u in range(2):
            c0 = 0
            for k, w in enumerate(LOAD_WIDTHS[u]):
                raw = keep.tile([P, 2, w], F32, name="raw%d_%d" % (u, k))
                nc.sync.dma_start(raw[:], pool_rows[u][:, :, c0:c0 + w])
                raws.append((u, k, c0, w, raw))
                c0 += w
                if (u, k) == (0, 0):
                    nc.sync.dma_start(ts_window[0:1, :], ts[0:1, :])
        q_raw = keep.tile([P, 4, NQ], F32, name="q_raw")
        nc.sync.dma_start(q_raw[:], qT[0].rearrange("(p t) n -> p t n", t=4))
        ch_sb = keep.tile([P, D], F32, name="ch_sb")
        nc.sync.dma_start(ch_sb[:], ch)

        ident = keep.tile([P, P], F32, name="ident")
        make_identity(nc, ident[:])
        warm = keep.tile([P, 8], F32, name="warm")
        nc.vector.memset(warm[:], 0.0)
        warm_out = keep.tile([P, 8], F32, name="warm_out")
        nc.scalar.activation(warm_out[:], warm[:], ACT.Exp)

        ts_part = keep.tile([P, PASSES, 4], F32, name="ts_part")
        ts_free = keep.tile([P, N], F32, name="ts_free")

        def token_scales():
            ts_listed = rows.tile([P, N], F32, name="ts_listed", tag="row")
            ts_down = keep.tile([P, PASSES, 4], F32, name="ts_down")
            for g in range(PASSES):
                nc.vector.tensor_copy(
                    ts_listed[:, g * PASS:(g + 1) * PASS], ts_window[:].indirect(offsets[:, g * 32:(g + 1) * 32])
                )
            for g in range(PASSES):
                bank = turn.tile([P, 4, P], F32, name="bank", tag="turn")
                for c in range(4):
                    c0 = g * PASS + c * P
                    nc.tensor.transpose(bank[:, c, :], ts_listed[:, c0:c0 + P], ident[:])
                nc.scalar.copy(ts_down[:, g, :], bank[:, :, 0])
            for g in range(PASSES):
                bank = turn.tile([P, 4, P], F32, name="bank", tag="turn")
                for c in range(4):
                    nc.tensor.transpose(bank[:, c, :], ts_down[:, g, c:c + 1].to_broadcast([P, P]), ident[:])
                nc.scalar.copy(
                    ts_free[:, g * PASS:(g + 1) * PASS].rearrange("p (j b r) -> p j b r", j=4, r=8),
                    bank[:].rearrange("p c (x j r) -> p j (c x) r", j=4, r=8),
                )
            for g in range(PASSES):
                bank = turn.tile([P, 4, P], F32, name="bank", tag="turn")
                for j in range(4):
                    c0 = g * PASS + j * P
                    nc.tensor.transpose(bank[:, j, :], ts_free[:, c0:c0 + P], ident[:])
                nc.scalar.copy(ts_part[:, g, :], bank[:, :, 0])

        windows = [keep.tile([P, 2 * T], BF16, name="window%d" % u, align_bytes=64) for u in range(2)]
        listed = keep.tile([P, 2, N], U32, name="listed")
        v_codes = keep.tile([P, PASSES, D], U32, name="v_codes", align_bytes=64)
        v_scales = keep.tile([P, PASSES, D], U8, name="v_scales", align_bytes=64)

        def cast(u, first, last):
            pairs = windows[u][:].rearrange("p (c i h) -> p c h i", i=2, h=2)
            for ru, k, c0, w, raw in raws:
                if ru == u and first <= k < last:
                    cut = w // 2 * VECTOR_SHARE[u][k] // 16
                    src = raw[:].rearrange("p h (c i) -> p c h i", i=2)
                    dst = pairs[:, c0 // 2:(c0 + w) // 2]
                    if cut > 0:
                        nc.vector.tensor_copy(dst[:, 0:cut], src[:, 0:cut])
                    if cut < w // 2:
                        nc.scalar.copy(dst[:, cut:], src[:, cut:])

        def gather(u, g):
            nc.vector.tensor_copy(
                listed[:, u, g * PASS:(g + 1) * PASS].rearrange("p (j b r) -> p b j r", j=4, r=8),
                windows[u][:].bitcast(U32).indirect(offsets[:, g * 32:(g + 1) * 32]),
            )

        def turn_values(u, g):
            bank = turn.tile([P, 4, P], F32, name="bank", tag="turn")
            words = listed[:, u, :].bitcast(F32)
            for j in range(4):
                c = g * PASS + j * P
                nc.tensor.transpose(bank[:, j, :], words[:, c:c + P], ident[:])
            v_bf = stage.tile([P, 2 * P, 4], BF16, name="v_bf", tag="stage", align_bytes=64)
            nc.scalar.copy(v_bf[:], bank[:].bitcast(BF16).rearrange("s j e -> s e j"))
            return v_bf

        def quantise_values(u, g, v_bf):
            cols = slice(u * 2 * P, (u + 1) * 2 * P)
            nc.vector.quantize_mx(
                out=v_codes[:, g, cols].bitcast(FP8X4),
                scales=v_scales[:, g, cols],
                in_=v_bf[:].rearrange("s e j -> s (e j)"),
            )

        token_scales()
        cast(0, 0, 9)
        for g in range(PASSES):
            gather(0, g)
        for k in range(len(LOAD_WIDTHS[1]) + 1):
            for g in range(PASSES):
                if VALUES_BEFORE[g] == k:
                    quantise_values(0, g, turn_values(0, g))
            cast(1, k, k + 1)
        for g in range(PASSES):
            gather(1, g)

        q_bf = keep.tile([P, NQ, 4], BF16, name="q_bf", align_bytes=64)
        nc.scalar.copy(
            q_bf[:].rearrange("p (c i) t -> p c t i", i=2), q_raw[:].rearrange("p t (c i) -> p c t i", i=2)
        )
        q_codes = keep.tile([P, NQ], U32, name="q_codes", tag="window1", align_bytes=64)
        q_scales = keep.tile([P, NQ], U8, name="q_scales", align_bytes=64)
        nc.vector.quantize_mx(
            out=q_codes[:].bitcast(FP8X4), scales=q_scales[:], in_=q_bf[:].rearrange("p n t -> p (n t)")
        )

        k_codes = keep.tile([P, N], U32, name="k_codes", align_bytes=64)
        k_scales = keep.tile([P, N], U8, name="k_scales", align_bytes=64)
        a = rows.tile([P, N], F32, name="a", tag="row")
        p = rows.tile([P, N], F32, name="p", tag="row")
        neg_max = keep.tile([P, PASSES], F32, name="neg_max")
        s_banks = []

        def scores(g):
            cols = slice(g * PASS, (g + 1) * PASS)
            k_words = stage.tile([P, PASS, 2], U32, name="k_words", tag="stage", align_bytes=64)
            nc.scalar.copy(
                k_words[:].rearrange("p (c i) u -> p c u i", i=2),
                listed[:, :, cols].rearrange("p u (c i) -> p c u i", i=2),
            )
            nc.vector.quantize_mx(
                out=k_codes[:, cols].bitcast(FP8X4),
                scales=k_scales[:, cols],
                in_=k_words[:].rearrange("p s u -> p (s u)").bitcast(BF16),
            )
            s_bank = score.tile([P, PASS], F32, name="s_bank")
            nc.tensor.matmul_mx(
                out=s_bank[:],
                lhsT=q_codes[:].bitcast(FP8X4),
                lhsT_scale=q_scales[:],
                rhs=k_codes[:, cols].bitcast(FP8X4),
                rhs_scale=k_scales[:, cols],
                start=True,
                stop=True,
            )
            s_banks.append(s_bank)

        def scale_scores(g):
            cols = slice(g * PASS, (g + 1) * PASS)
            nc.vector.tensor_tensor(a[:, cols], s_banks[g][:], ts_free[:, cols], ALU.mult)

        def row_max(g):
            cols = slice(g * PASS, (g + 1) * PASS)
            nc.vector.tensor_scalar(
                out=p[:, cols],
                in0=a[:, cols],
                scalar1=-1.0,
                scalar2=neg_max[:, g - 1:g] if g else None,
                op0=ALU.mult,
                op1=ALU.min,
                accum_out=neg_max[:, g:g + 1],
            )

        scores(0)
        scores(1)
        scores(2)
        scale_scores(0)
        scores(3)
        for g in range(1, PASSES):
            scale_scores(g)
            row_max(g - 1)
        row_max(PASSES - 1)

        sums = keep.tile([P, PASSES], F32, name="sums")
        for g in range(PASSES):
            cols = slice(g * PASS, (g + 1) * PASS)
            nc.scalar.activation(
                p[:, cols], a[:, cols], ACT.Exp, bias=neg_max[:, PASSES - 1:PASSES], accum_out=sums[:, g:g + 1]
            )
        for g in range(PASSES):
            quantise_values(1, g, turn_values(1, g))

        total = keep.tile([P, 1], F32, name="total")
        nc.vector.tensor_reduce(total[:], sums[:], AX.X, ALU.add)
        inverse = keep.tile([P, 1], F32, name="inverse")
        nc.vector.reciprocal(inverse[:], total[:])
        factor = keep.tile([P, D], F32, name="factor")
        nc.scalar.activation(factor[:], ch_sb[:], ACT.Copy, scale=inverse[:])

        w_codes = keep.tile([P, PASSES, NQ], U32, name="w_codes", align_bytes=64)
        w_scales = keep.tile([P, PASSES, NQ], U8, name="w_scales", align_bytes=64)
        y = acc.tile([P, D], F32, name="y")
        w_tiles = []

        def weights(g):
            bank = turn.tile([P, 4, P], F32, name="bank", tag="turn")
            for j in range(4):
                c = g * PASS + j * P
                nc.tensor.transpose(bank[:, j, :], p[:, c:c + P], ident[:])
            w_bf = ring.tile([P, NQ, 4], BF16, name="w_bf", align_bytes=64)
            nc.vector.tensor_tensor(
                w_bf[:],
                bank[:].rearrange("s j q -> s q j"),
                ts_part[:, g:g + 1, :].to_broadcast([P, NQ, 4]),
                ALU.mult,
            )
            w_tiles.append(w_bf)

        def weighted_sum(g):
            nc.vector.quantize_mx(
                out=w_codes[:, g, :].bitcast(FP8X4),
                scales=w_scales[:, g, :],
                in_=w_tiles[g][:].rearrange("s q j -> s (q j)"),
            )
            nc.tensor.matmul_mx(
                out=y[:],
                lhsT=w_codes[:, g, :].bitcast(FP8X4),
                lhsT_scale=w_scales[:, g, :],
                rhs=v_codes[:, g, :].bitcast(FP8X4),
                rhs_scale=v_scales[:, g, :],
                start=(g == 0),
                stop=(g == PASSES - 1),
            )

        weights(0)
        for g in range(1, PASSES):
            weights(g)
            weighted_sum(g - 1)
        weighted_sum(PASSES - 1)

        result = keep.tile([P, D], F32, name="result")
        nc.vector.tensor_tensor(
            result[:].rearrange("q (c u h) -> q c u h", u=2, h=2),
            y[:].rearrange("q (u c h) -> q c u h", u=2, h=2),
            factor[:].rearrange("q (c u h) -> q c u h", u=2, h=2),
            ALU.mult,
        )
        nc.sync.dma_start(out[0], result[:])
